import numpy as np
import ml_dtypes


def mxq(x, axis, fmt="e4m3"):
    dtype, down = {"e4m3": (ml_dtypes.float8_e4m3fn, 7), "e5m2": (ml_dtypes.float8_e5m2, 14)}[fmt]
    v = np.moveaxis(np.asarray(x, np.float32).astype(ml_dtypes.bfloat16).astype(np.float64), axis, -1)
    blocks = v.reshape(v.shape[:-1] + (-1, 32))
    amax = np.abs(blocks).max(-1, keepdims=True)
    byte = np.maximum(np.where(amax > 0, np.frexp(amax)[1] - 1 + 127, 0) - down, 1)
    scale = np.exp2(byte - 127.0)
    codes = (blocks / scale).astype(np.float32).astype(dtype).astype(np.float64)
    return np.moveaxis((codes * scale).reshape(v.shape), -1, axis)


WIDE = False


def mx_kscale(k):
    if not WIDE:
        return np.ones(k)
    levels = np.array([10, -10, 5, -5, 0])
    if k % 512:
        return np.exp2(np.random.permutation(np.resize(levels, k // 32))).repeat(32)
    a = np.empty((k // 512, 16))
    for p in range(k // 512):
        a[p, :8] = np.random.permutation(np.resize(levels, 8))
        for g in range(8):
            far = levels[np.abs(levels - a[p, g]) >= 10]
            a[p, g + 8] = far[np.random.randint(len(far))]
    return np.exp2(a.ravel()).repeat(32)


BF16 = ml_dtypes.bfloat16


def bf(x):
    return np.asarray(x, np.float32).astype(BF16)


def f64(x):
    return np.asarray(x).astype(np.float64)

E4M3FN = np.array([(-1.0 if i & 128 else 1.0) * ((1.0 + (i & 7) / 8.0) * 2.0 ** (((i >> 3) & 15) - 7) if i & 120 else (i & 7) * 2.0 ** -9) for i in range(256)])


def e4m3fn_bytes(y):
    return np.clip(np.asarray(y, np.float64), -448.0, 448.0).astype(np.float32).astype(ml_dtypes.float8_e4m3fn).view(np.uint8)


def e4m3fn_values(b):
    return E4M3FN[b]


T, F, D = 1024, 2048, 1536


def setup_inputs():
    s = mx_kscale(F)
    w = np.random.standard_normal((F, D)) / np.sqrt(F) / s[:, None]
    w_scale = (np.abs(w).max(axis=1, keepdims=True) / 448).astype(np.float32)
    return {"gate": bf(np.random.standard_normal((T, F))),
            "up": bf(1.5 * np.random.standard_normal((T, F)) * s),
            "router": bf(np.random.standard_normal(T)),
            "w_bytes": e4m3fn_bytes(w / w_scale.astype(np.float64)),
            "w_scale": w_scale}


def reference(gate, up, router, w_bytes, w_scale):
    a = f64(gate)
    h = a / (1 + np.exp(-a)) * f64(up)
    w = e4m3fn_values(w_bytes) * np.repeat(f64(w_scale), D, axis=1)
    y = mxq(h, 1, "e4m3") @ mxq(w, 0, "e4m3")
    r = 1 / (1 + np.exp(-f64(router)))
    return y * r[:, None]

@@ -1,0 +1,162 @@
+from contextlib import ExitStack
+
+import concourse.mybir as mybir
+from concourse.masks import make_identity
+
+T, F, D = 1024, 2048, 1536
+FLOPS = 2 * T * F * D
+
+F32 = mybir.dt.float32
+BF16 = mybir.dt.bfloat16
+U32 = mybir.dt.uint32
+U8 = mybir.dt.uint8
+FP8 = mybir.dt.float8_e4m3fn
+FP8X4 = mybir.dt.float8_e4m3fn_x4
+ACT = mybir.ActivationFunctionType
+MULT = mybir.AluOpType.mult
+
+P = 128
+G = F // 512
+NT = T // P
+SLICES = [(0, 512), (512, 512), (1024, 256), (1280, 256)]
+ORDER = "s0 h0 h1 h2 h3 h4 h5 s1 h6 s2 h7 s3".split(" ")
+SCALAR_COLS = [512, 512, 128, 0]
+
+
+def tile_gated_expert_down_d3_kernel(tc, gate, up, router, w_bytes, w_scale, out):
+    nc = tc.nc
+    with ExitStack() as ctx:
+        keep = ctx.enter_context(tc.tile_pool(name="keep", bufs=1))
+        work = ctx.enter_context(tc.tile_pool(name="work", bufs=4))
+        psum = ctx.enter_context(tc.psum_pool(name="psum", bufs=2))
+
+        gate_rows = gate.rearrange("(p i) f -> i p f", i=NT)
+        up_rows = up.rearrange("(p i) f -> i p f", i=NT)
+        out_rows = out.rearrange("(p i) d -> i p d", i=NT)
+        w_rows = w_bytes.rearrange("(g p t) n -> g p t n", p=P, t=4)
+
+        ws = keep.tile([P, G, 4], F32, name="ws")
+        ws_src = w_scale.rearrange("(g p t) o -> p g (t o)", p=P, t=4)
+        nc.scalar.dma_start(out=ws[:], in_=ws_src)
+        r_in = keep.tile([P, NT], BF16, name="r_in")
+        nc.scalar.dma_start(out=r_in[:], in_=router.rearrange("(p i) -> p i", i=NT))
+        r = keep.tile([P, NT], F32, name="r")
+        nc.scalar.activation(out=r[:], in_=r_in[:], func=ACT.Sigmoid)
+
+        ident = keep.tile([P, P], F32, name="ident")
+        make_identity(nc, ident[:])
+
+        g_sb, u_sb, w_sb = [], [], []
+        for i in range(NT):
+            g_sb.append(keep.tile([P, F], BF16, name="gate%d" % i))
+            u_sb.append(keep.tile([P, F], BF16, name="up%d" % i))
+        for g in range(G):
+            w_sb.append(keep.tile([P, 4, D], U8, name="wbytes%d" % g))
+
+        def load_w(g, a):
+            nc.sync.dma_start(out=w_sb[g][:, 2 * a : 2 * a + 2, :], in_=w_rows[g][:, 2 * a : 2 * a + 2, :])
+
+        def load_tok(dst, src, i, j):
+            nc.sync.dma_start(out=dst[i][:, 1024 * j : 1024 * (j + 1)], in_=src[i][:, 1024 * j : 1024 * (j + 1)])
+
+        load_tok(g_sb, gate_rows, 0, 0)
+        load_w(0, 0)
+        load_tok(u_sb, up_rows, 0, 0)
+        load_w(0, 1)
+        load_tok(g_sb, gate_rows, 0, 1)
+        load_tok(u_sb, up_rows, 0, 1)
+        for g in range(1, G):
+            load_w(g, 0)
+            load_w(g, 1)
+        for i in range(1, NT):
+            for j in range(2):
+                load_tok(g_sb, gate_rows, i, j)
+                load_tok(u_sb, up_rows, i, j)
+
+        h_codes, h_scales, w_codes, w_scales = [], [], [], []
+        for i in range(NT):
+            h_codes.append(keep.tile([P, 512], U32, name="hcodes%d" % i, align_bytes=64))
+            h_scales.append(keep.tile([P, 512], U8, name="hscales%d" % i, align_bytes=64))
+        for s in range(len(SLICES)):
+            w_codes.append(keep.tile([P, G, SLICES[s][1]], U32, name="wcodes%d" % s, align_bytes=64))
+            w_scales.append(keep.tile([P, G, SLICES[s][1]], U8, name="wscales%d" % s, align_bytes=64))
+
+        def turn(src, i, j, tag):
+            bank = psum.tile([P, 2, 256], F32, name=tag, bufs=2)
+            words = src[i][:].bitcast(F32)
+            for q in range(2):
+                g = 2 * j + q
+                for u in range(2):
+                    nc.tensor.transpose(
+                        bank[:, u, 128 * q : 128 * (q + 1)], words[:, 256 * g + u : 256 * (g + 1) : 2], ident[:]
+                    )
+            return bank[:].bitcast(BF16).rearrange("p u (x e) -> p x u e", e=2)
+
+        def hidden(i):
+            h = work.tile([P, 2048], BF16, name="h", bufs=2, align_bytes=64)
+            for j in range(2):
+                gt = turn(g_sb, i, j, "tg")
+                ut = turn(u_sb, i, j, "tu")
+                sil = work.tile([P, 1024], F32, name="sil", bufs=4)
+                silv = sil[:].rearrange("p (x u e) -> p x u e", u=2, e=2)
+                nc.scalar.activation(out=silv, in_=gt, func=ACT.Silu)
+                hv = h[:, 1024 * j : 1024 * (j + 1)].rearrange("p (x u e) -> p x u e", u=2, e=2)
+                nc.vector.tensor_tensor(out=hv, in0=silv, in1=ut, op=MULT)
+            nc.vector.quantize_mx(out=h_codes[i][:].bitcast(FP8X4), scales=h_scales[i][:], in_=h[:])
+
+        def weights(s):
+            n0, nw = SLICES[s]
+            for g in range(G):
+                pairs = work.tile([P, 2, nw, 2], BF16, name="pairs", bufs=4)
+                for t in range(4):
+                    nc.vector.tensor_scalar(
+                        out=pairs[:, t // 2, :, t % 2],
+                        in0=w_sb[g][:, t, n0 : n0 + nw].bitcast(FP8),
+                        scalar1=ws[:, g, t : t + 1],
+                        scalar2=None,
+                        op0=MULT,
+                    )
+                mixed = work.tile([P, nw, 4], BF16, name="mixed", bufs=4, align_bytes=64)
+                src = pairs[:].rearrange("p u n e -> p (u n e)").bitcast(F32).rearrange("p (u n) -> p n u", u=2)
+                dst = mixed[:].rearrange("p n t -> p (n t)").bitcast(F32).rearrange("p (n u) -> p n u", u=2)
+                c = SCALAR_COLS[s]
+                if c > 0:
+                    nc.scalar.copy(out=dst[:, :c, :], in_=src[:, :c, :])
+                if c < nw:
+                    nc.vector.tensor_copy(out=dst[:, c:, :], in_=src[:, c:, :])
+                nc.vector.quantize_mx(
+                    out=w_codes[s][:, g, :].bitcast(FP8X4),
+                    scales=w_scales[s][:, g, :],
+                    in_=mixed[:].rearrange("p n t -> p (n t)"),
+                )
+
+        def product(i, s):
+            n0, nw = SLICES[s]
+            acc = psum.tile([P, 512], F32, name="acc", bufs=4)
+            for g in range(G):
+                nc.tensor.matmul_mx(
+                    out=acc[:, :nw],
+                    lhsT=h_codes[i][:, 128 * g : 128 * (g + 1)].bitcast(FP8X4),
+                    lhsT_scale=h_scales[i][:, 128 * g : 128 * (g + 1)],
+                    rhs=w_codes[s][:, g, :].bitcast(FP8X4),
+                    rhs_scale=w_scales[s][:, g, :],
+                    start=(g == 0),
+                    stop=(g == G - 1),
+                )
+            res = work.tile([P, 512], F32, name="res", bufs=6)
+            nc.scalar.activation(out=res[:, :nw], in_=acc[:, :nw], func=ACT.Copy, scale=r[:, i : i + 1])
+            nc.sync.dma_start(out=out_rows[i][:, n0 : n0 + nw], in_=res[:, :nw])
+
+        ready_h, ready_s = [], []
+        for item in ORDER:
+            k = int(item[1:])
+            if item.startswith("h"):
+                hidden(k)
+                ready_h.append(k)
+                for s in ready_s:
+                    product(k, s)
+            else:
+                weights(k)
+                ready_s.append(k)
+                for i in ready_h:
+                    product(i, k)

@@ -19,13 +19,22 @@ P = 128
 G = F // 512
 NT = T // P
 SLICES = [(0, 512), (512, 512), (1024, 256), (1280, 256)]
-ORDER = "s0 h0 h1 h2 h3 h4 h5 s1 h6 s2 h7 s3".split(" ")
-SCALAR_COLS = [512, 512, 128, 0]
+STEPS = (
+    "w00 k0 w01 w02 k1 w03 k2 w10 k3 w11 k4 k5 k6 k7 k8 k9 k10 k11 w12 k12 w13 w20 k13 w21 k14 w22 w23 k15 w30 w31 w32 w33"
+).split(" ")
+SCALAR_COLS = [416,320,32,0]
+SCALAR_EXITS = 100
+TURN_AHEAD = 2
+SILU_AHEAD = 1
+EXIT_LAG = 2
+PRODUCTS_AT_K = 0
+PRODUCTS_AT_W = 3
 
 
 def tile_gated_expert_down_d3_kernel(tc, gate, up, router, w_bytes, w_scale, out):
     nc = tc.nc
     with ExitStack() as ctx:
+        ctx.enter_context(tc.manual_schedule())
         keep = ctx.enter_context(tc.tile_pool(name="keep", bufs=1))
         work = ctx.enter_context(tc.tile_pool(name="work", bufs=4))
         psum = ctx.enter_context(tc.psum_pool(name="psum", bufs=2))
@@ -92,43 +101,61 @@ def tile_gated_expert_down_d3_kernel(tc, gate, up, router, w_bytes, w_scale, out
                     )
             return bank[:].bitcast(BF16).rearrange("p u (x e) -> p x u e", e=2)
 
-        def hidden(i):
-            h = work.tile([P, 2048], BF16, name="h", bufs=2, align_bytes=64)
-            for j in range(2):
-                gt = turn(g_sb, i, j, "tg")
-                ut = turn(u_sb, i, j, "tu")
-                sil = work.tile([P, 1024], F32, name="sil", bufs=4)
-                silv = sil[:].rearrange("p (x u e) -> p x u e", u=2, e=2)
-                nc.scalar.activation(out=silv, in_=gt, func=ACT.Silu)
-                hv = h[:, 1024 * j : 1024 * (j + 1)].rearrange("p (x u e) -> p x u e", u=2, e=2)
-                nc.vector.tensor_tensor(out=hv, in0=silv, in1=ut, op=MULT)
-            nc.vector.quantize_mx(out=h_codes[i][:].bitcast(FP8X4), scales=h_scales[i][:], in_=h[:])
+        live = {}
 
-        def weights(s):
+        def turn_half(k):
+            i, j = divmod(k, 2)
+            live["g", k] = turn(g_sb, i, j, "tg")
+            live["u", k] = turn(u_sb, i, j, "tu")
+
+        def silu_half(k):
+            sil = work.tile([P, 1024], F32, name="sil", bufs=4)
+            silv = sil[:].rearrange("p (x u e) -> p x u e", u=2, e=2)
+            nc.scalar.activation(out=silv, in_=live.pop(("g", k)), func=ACT.Silu)
+            live["s", k] = silv
+
+        def prod_half(k):
+            i, j = divmod(k, 2)
+            if j == 0:
+                h = work.tile([P, 2048], BF16, name="h", bufs=2, align_bytes=64)
+                live["h", i] = h
+            hv = live["h", i][:, 1024 * j : 1024 * (j + 1)].rearrange("p (x u e) -> p x u e", u=2, e=2)
+            nc.vector.tensor_tensor(out=hv, in0=live.pop(("s", k)), in1=live.pop(("u", k)), op=MULT)
+
+        def quantize_hidden(i):
+            nc.vector.quantize_mx(
+                out=h_codes[i][:].bitcast(FP8X4), scales=h_scales[i][:], in_=live.pop(("h", i))[:]
+            )
+
+        def widen(s, g):
             n0, nw = SLICES[s]
-            for g in range(G):
-                pairs = work.tile([P, 2, nw, 2], BF16, name="pairs", bufs=4)
-                for t in range(4):
-                    nc.vector.tensor_scalar(
-                        out=pairs[:, t // 2, :, t % 2],
-                        in0=w_sb[g][:, t, n0 : n0 + nw].bitcast(FP8),
-                        scalar1=ws[:, g, t : t + 1],
-                        scalar2=None,
-                        op0=MULT,
-                    )
-                mixed = work.tile([P, nw, 4], BF16, name="mixed", bufs=4, align_bytes=64)
-                src = pairs[:].rearrange("p u n e -> p (u n e)").bitcast(F32).rearrange("p (u n) -> p n u", u=2)
-                dst = mixed[:].rearrange("p n t -> p (n t)").bitcast(F32).rearrange("p (n u) -> p n u", u=2)
-                c = SCALAR_COLS[s]
-                if c > 0:
-                    nc.scalar.copy(out=dst[:, :c, :], in_=src[:, :c, :])
-                if c < nw:
-                    nc.vector.tensor_copy(out=dst[:, c:, :], in_=src[:, c:, :])
-                nc.vector.quantize_mx(
-                    out=w_codes[s][:, g, :].bitcast(FP8X4),
-                    scales=w_scales[s][:, g, :],
-                    in_=mixed[:].rearrange("p n t -> p (n t)"),
+            planes = work.tile([P, 4, nw], BF16, name="planes", bufs=3)
+            for t in range(4):
+                nc.vector.tensor_scalar(
+                    out=planes[:, t, :],
+                    in0=w_sb[g][:, t, n0 : n0 + nw].bitcast(FP8),
+                    scalar1=ws[:, g, t : t + 1],
+                    scalar2=None,
+                    op0=MULT,
                 )
+            mixed = work.tile([P, nw, 4], BF16, name="mixed", bufs=4, align_bytes=64)
+            live["p", s, g] = planes
+            live["m", s, g] = mixed
+
+        def interleave(s, g, c0, c1, copy):
+            planes, mixed = live["p", s, g], live["m", s, g]
+            copy(
+                out=mixed[:, c0:c1, :].rearrange("p (c i) t -> p c t i", i=4),
+                in_=planes[:, :, c0:c1].rearrange("p t (c i) -> p c t i", i=4),
+            )
+
+        def quantize_weights(s, g):
+            mixed = live.pop(("m", s, g))
+            nc.vector.quantize_mx(
+                out=w_codes[s][:, g, :].bitcast(FP8X4),
+                scales=w_scales[s][:, g, :],
+                in_=mixed[:].rearrange("p n t -> p (n t)"),
+            )
 
         def product(i, s):
             n0, nw = SLICES[s]
@@ -143,20 +170,81 @@ def tile_gated_expert_down_d3_kernel(tc, gate, up, router, w_bytes, w_scale, out
                     start=(g == 0),
                     stop=(g == G - 1),
                 )
+            return acc
+
+        exit_count = [0]
+
+        def finish(i, s, acc):
+            n0, nw = SLICES[s]
             res = work.tile([P, 512], F32, name="res", bufs=6)
-            nc.scalar.activation(out=res[:, :nw], in_=acc[:, :nw], func=ACT.Copy, scale=r[:, i : i + 1])
+            if exit_count[0] < SCALAR_EXITS or exit_count[0] % 2 == 0:
+                nc.scalar.activation(out=res[:, :nw], in_=acc[:, :nw], func=ACT.Copy, scale=r[:, i : i + 1])
+            else:
+                nc.vector.tensor_scalar(
+                    out=res[:, :nw], in0=acc[:, :nw], scalar1=r[:, i : i + 1], scalar2=None, op0=MULT
+                )
+            exit_count[0] += 1
             nc.sync.dma_start(out=out_rows[i][:, n0 : n0 + nw], in_=res[:, :nw])
 
-        ready_h, ready_s = [], []
-        for item in ORDER:
-            k = int(item[1:])
-            if item.startswith("h"):
-                hidden(k)
-                ready_h.append(k)
-                for s in ready_s:
-                    product(k, s)
-            else:
-                weights(k)
-                ready_s.append(k)
-                for i in ready_h:
-                    product(i, k)
+        turned, silued, seen = 0, 0, 0
+        hidden_done, slices_done, ready, open_banks = [], [], [], []
+        quantized = [0] * len(SLICES)
+        later = []
+
+        def run_products(n):
+            for pair in ready[:n]:
+                open_banks.append((pair, product(*pair)))
+                while len(open_banks) > EXIT_LAG:
+                    pair2, acc = open_banks.pop(0)
+                    finish(*pair2, acc)
+            del_n = ready[n:]
+            ready.clear()
+            ready.extend(del_n)
+
+        def end_hidden(i):
+            quantize_hidden(i)
+            hidden_done.append(i)
+            ready.extend([(i, s) for s in slices_done])
+
+        def end_weights(s, g):
+            quantize_weights(s, g)
+            quantized[s] += 1
+            if quantized[s] == G:
+                slices_done.append(s)
+                ready.extend([(i, s) for i in hidden_done])
+
+        for n, step in enumerate(STEPS + ["-"] * 2):
+            due = [x for x in later if x[0] <= n]
+            later = [x for x in later if x[0] > n]
+            is_k = step.startswith("k")
+            if step != "-":
+                k = int(step[1:]) if is_k else -1
+                want = min(2 * NT, max(seen + SILU_AHEAD, k + 1))
+                while turned < min(2 * NT, max(seen + TURN_AHEAD, want)):
+                    turn_half(turned)
+                    turned += 1
+                while silued < want:
+                    silu_half(silued)
+                    silued += 1
+            if is_k:
+                prod_half(k)
+                seen = k + 1
+                if k % 2 == 1:
+                    later.append((n + 1, end_hidden, (k // 2,)))
+            elif step != "-":
+                s, g = int(step[1:2]), int(step[2:])
+                nw = SLICES[s][1]
+                widen(s, g)
+                c = SCALAR_COLS[s]
+                if c > 0:
+                    interleave(s, g, 0, c, nc.scalar.copy)
+                if c < nw:
+                    later.append((n + 1, interleave, (s, g, c, nw, nc.vector.tensor_copy)))
+                later.append((n + 2, end_weights, (s, g)))
+            for x in due:
+                x[1](*x[2])
+            run_products(PRODUCTS_AT_K if is_k else PRODUCTS_AT_W)
+        run_products(len(ready))
+        while open_banks:
+            pair2, acc = open_banks.pop(0)
+            finish(*pair2, acc)

@@ -20,15 +20,15 @@ G = F // 512
 NT = T // P
 SLICES = [(0, 512), (512, 512), (1024, 256), (1280, 256)]
 STEPS = (
-    "w00 k0 w01 w02 k1 w03 k2 w10 k3 w11 k4 k5 k6 k7 k8 k9 k10 k11 w12 k12 w13 w20 k13 w21 k14 w22 w23 k15 w30 w31 w32 w33"
+    "w00 w01 w02 k0 k1 w03 k2 k3 k4 w10 k5 k6 w11 k7 k8 w12 k9 w13 k10 k11 w20 k12 w21 k13 w22 w23 w30 k14 w31 k15 w32 w33"
 ).split(" ")
-SCALAR_COLS = [416,320,32,0]
-SCALAR_EXITS = 100
-TURN_AHEAD = 2
-SILU_AHEAD = 1
-EXIT_LAG = 2
+SCALAR_COLS = [384,384,128,0]
+SCALAR_EXITS = 24
+TURN_AHEAD = 1
+SILU_AHEAD = 2
+EXIT_LAG = 1
 PRODUCTS_AT_K = 0
-PRODUCTS_AT_W = 3
+PRODUCTS_AT_W = 1
 
 
 def tile_gated_expert_down_d3_kernel(tc, gate, up, router, w_bytes, w_scale, out):
@@ -109,7 +109,7 @@ def tile_gated_expert_down_d3_kernel(tc, gate, up, router, w_bytes, w_scale, out
             live["u", k] = turn(u_sb, i, j, "tu")
 
         def silu_half(k):
-            sil = work.tile([P, 1024], F32, name="sil", bufs=4)
+            sil = work.tile([P, 1024], F32, name="sil", bufs=6)
             silv = sil[:].rearrange("p (x u e) -> p x u e", u=2, e=2)
             nc.scalar.activation(out=silv, in_=live.pop(("g", k)), func=ACT.Silu)
             live["s", k] = silv
@@ -129,7 +129,7 @@ def tile_gated_expert_down_d3_kernel(tc, gate, up, router, w_bytes, w_scale, out
 
         def widen(s, g):
             n0, nw = SLICES[s]
-            planes = work.tile([P, 4, nw], BF16, name="planes", bufs=3)
+            planes = work.tile([P, 4, nw], BF16, name="planes", bufs=5)
             for t in range(4):
                 nc.vector.tensor_scalar(
                     out=planes[:, t, :],
@@ -138,7 +138,7 @@ def tile_gated_expert_down_d3_kernel(tc, gate, up, router, w_bytes, w_scale, out
                     scalar2=None,
                     op0=MULT,
                 )
-            mixed = work.tile([P, nw, 4], BF16, name="mixed", bufs=4, align_bytes=64)
+            mixed = work.tile([P, nw, 4], BF16, name="mixed", bufs=5, align_bytes=64)
             live["p", s, g] = planes
             live["m", s, g] = mixed
 
@@ -213,7 +213,7 @@ def tile_gated_expert_down_d3_kernel(tc, gate, up, router, w_bytes, w_scale, out
                 slices_done.append(s)
                 ready.extend([(i, s) for i in hidden_done])
 
-        for n, step in enumerate(STEPS + ["-"] * 2):
+        for n, step in enumerate(STEPS + ["-"] * 3):
             due = [x for x in later if x[0] <= n]
             later = [x for x in later if x[0] > n]
             is_k = step.startswith("k")
@@ -230,7 +230,7 @@ def tile_gated_expert_down_d3_kernel(tc, gate, up, router, w_bytes, w_scale, out
                 prod_half(k)
                 seen = k + 1
                 if k % 2 == 1:
-                    later.append((n + 1, end_hidden, (k // 2,)))
+                    later.append((n + 2, end_hidden, (k // 2,)))
             elif step != "-":
                 s, g = int(step[1:2]), int(step[2:])
                 nw = SLICES[s][1]
@@ -240,7 +240,7 @@ def tile_gated_expert_down_d3_kernel(tc, gate, up, router, w_bytes, w_scale, out
                     interleave(s, g, 0, c, nc.scalar.copy)
                 if c < nw:
                     later.append((n + 1, interleave, (s, g, c, nw, nc.vector.tensor_copy)))
-                later.append((n + 2, end_weights, (s, g)))
+                later.append((n + 3, end_weights, (s, g)))
             for x in due:
                 x[1](*x[2])
             run_products(PRODUCTS_AT_K if is_k else PRODUCTS_AT_W)

@@ -18,17 +18,17 @@ MULT = mybir.AluOpType.mult
 P = 128
 G = F // 512
 NT = T // P
-SLICES = [(0, 512), (512, 512), (1024, 256), (1280, 256)]
+SLICES = [(0, 512), (512, 256), (768, 256), (1024, 256), (1280, 256)]
 STEPS = (
-    "w00 w01 w02 k0 k1 w03 k2 k3 k4 w10 k5 k6 w11 k7 k8 w12 k9 w13 k10 k11 w20 k12 w21 k13 w22 w23 w30 k14 w31 k15 w32 w33"
+    "w00 w01 k0 k1 w02 w03 k2 k3 w10 w11 k4 k5 w12 w13 k6 k7 w20 k8 w21 w22 k9 k10 w23 k11 k12 w30 w31 k13 k14 w32 w33 k15 w40 w41 w42 w43"
 ).split(" ")
-SCALAR_COLS = [384,384,128,0]
-SCALAR_EXITS = 24
-TURN_AHEAD = 1
+SCALAR_COLS = [416,160,128,192,96]
+SCALAR_EXITS = 100
+TURN_AHEAD = 2
 SILU_AHEAD = 2
-EXIT_LAG = 1
+EXIT_LAG = 0
 PRODUCTS_AT_K = 0
-PRODUCTS_AT_W = 1
+PRODUCTS_AT_W = 3
 
 
 def tile_gated_expert_down_d3_kernel(tc, gate, up, router, w_bytes, w_scale, out):
@@ -62,25 +62,33 @@ def tile_gated_expert_down_d3_kernel(tc, gate, up, router, w_bytes, w_scale, out
         for g in range(G):
             w_sb.append(keep.tile([P, 4, D], U8, name="wbytes%d" % g))
 
-        def load_w(g, a):
-            nc.sync.dma_start(out=w_sb[g][:, 2 * a : 2 * a + 2, :], in_=w_rows[g][:, 2 * a : 2 * a + 2, :])
+        def load_w(g, n0, n1):
+            nc.sync.dma_start(out=w_sb[g][:, :, n0:n1], in_=w_rows[g][:, :, n0:n1])
 
-        def load_tok(dst, src, i, j):
+        def load_half(dst, src, i, j):
             nc.sync.dma_start(out=dst[i][:, 1024 * j : 1024 * (j + 1)], in_=src[i][:, 1024 * j : 1024 * (j + 1)])
 
-        load_tok(g_sb, gate_rows, 0, 0)
-        load_w(0, 0)
-        load_tok(u_sb, up_rows, 0, 0)
-        load_w(0, 1)
-        load_tok(g_sb, gate_rows, 0, 1)
-        load_tok(u_sb, up_rows, 0, 1)
-        for g in range(1, G):
-            load_w(g, 0)
-            load_w(g, 1)
-        for i in range(1, NT):
-            for j in range(2):
-                load_tok(g_sb, gate_rows, i, j)
-                load_tok(u_sb, up_rows, i, j)
+        def load_tokens(i, j):
+            load_half(g_sb, gate_rows, i, j)
+            load_half(u_sb, up_rows, i, j)
+
+        load_w(0, 0, 512)
+        load_tokens(0, 0)
+        load_w(1, 0, 512)
+        load_tokens(0, 1)
+        load_w(2, 0, 512)
+        load_w(3, 0, 512)
+        load_tokens(1, 0)
+        load_tokens(1, 1)
+        load_w(0, 512, D)
+        load_w(1, 512, D)
+        load_tokens(2, 0)
+        load_tokens(2, 1)
+        load_w(2, 512, D)
+        load_w(3, 512, D)
+        for i in range(3, NT):
+            load_tokens(i, 0)
+            load_tokens(i, 1)
 
         h_codes, h_scales, w_codes, w_scales = [], [], [], []
         for i in range(NT):
@@ -109,7 +117,7 @@ def tile_gated_expert_down_d3_kernel(tc, gate, up, router, w_bytes, w_scale, out
             live["u", k] = turn(u_sb, i, j, "tu")
 
         def silu_half(k):
-            sil = work.tile([P, 1024], F32, name="sil", bufs=6)
+            sil = work.tile([P, 1024], F32, name="sil", bufs=4)
             silv = sil[:].rearrange("p (x u e) -> p x u e", u=2, e=2)
             nc.scalar.activation(out=silv, in_=live.pop(("g", k)), func=ACT.Silu)
             live["s", k] = silv
@@ -129,7 +137,7 @@ def tile_gated_expert_down_d3_kernel(tc, gate, up, router, w_bytes, w_scale, out
 
         def widen(s, g):
             n0, nw = SLICES[s]
-            planes = work.tile([P, 4, nw], BF16, name="planes", bufs=5)
+            planes = work.tile([P, 4, nw], BF16, name="planes", bufs=3)
             for t in range(4):
                 nc.vector.tensor_scalar(
                     out=planes[:, t, :],
@@ -138,7 +146,7 @@ def tile_gated_expert_down_d3_kernel(tc, gate, up, router, w_bytes, w_scale, out
                     scalar2=None,
                     op0=MULT,
                 )
-            mixed = work.tile([P, nw, 4], BF16, name="mixed", bufs=5, align_bytes=64)
+            mixed = work.tile([P, nw, 4], BF16, name="mixed", bufs=6, align_bytes=64)
             live["p", s, g] = planes
             live["m", s, g] = mixed
 
@@ -213,7 +221,7 @@ def tile_gated_expert_down_d3_kernel(tc, gate, up, router, w_bytes, w_scale, out
                 slices_done.append(s)
                 ready.extend([(i, s) for i in hidden_done])
 
-        for n, step in enumerate(STEPS + ["-"] * 3):
+        for n, step in enumerate(STEPS + ["-"] * 4):
             due = [x for x in later if x[0] <= n]
             later = [x for x in later if x[0] > n]
             is_k = step.startswith("k")
@@ -230,7 +238,7 @@ def tile_gated_expert_down_d3_kernel(tc, gate, up, router, w_bytes, w_scale, out
                 prod_half(k)
                 seen = k + 1
                 if k % 2 == 1:
-                    later.append((n + 2, end_hidden, (k // 2,)))
+                    later.append((n + 1, end_hidden, (k // 2,)))
             elif step != "-":
                 s, g = int(step[1:2]), int(step[2:])
                 nw = SLICES[s][1]
@@ -240,7 +248,7 @@ def tile_gated_expert_down_d3_kernel(tc, gate, up, router, w_bytes, w_scale, out
                     interleave(s, g, 0, c, nc.scalar.copy)
                 if c < nw:
                     later.append((n + 1, interleave, (s, g, c, nw, nc.vector.tensor_copy)))
-                later.append((n + 3, end_weights, (s, g)))
+                later.append((n + 4, end_weights, (s, g)))
             for x in due:
                 x[1](*x[2])
             run_products(PRODUCTS_AT_K if is_k else PRODUCTS_AT_W)

from contextlib import ExitStack

import concourse.mybir as mybir
from concourse.masks import make_identity

T, F, D = 1024, 2048, 1536
FLOPS = 2 * T * F * D

F32 = mybir.dt.float32
BF16 = mybir.dt.bfloat16
U32 = mybir.dt.uint32
U8 = mybir.dt.uint8
FP8 = mybir.dt.float8_e4m3fn
FP8X4 = mybir.dt.float8_e4m3fn_x4
ACT = mybir.ActivationFunctionType
MULT = mybir.AluOpType.mult

P = 128
G = F // 512
NT = T // P
SLICES = [(0, 512), (512, 256), (768, 256), (1024, 256), (1280, 256)]
STEPS = (
    "w00 w01 k0 k1 w02 w03 k2 k3 w10 w11 k4 k5 w12 w13 k6 k7 w20 k8 w21 w22 k9 k10 w23 k11 k12 w30 w31 k13 k14 w32 w33 k15 w40 w41 w42 w43"
).split(" ")
SCALAR_COLS = [416,160,128,192,96]
SCALAR_EXITS = 100
TURN_AHEAD = 2
SILU_AHEAD = 2
EXIT_LAG = 0
PRODUCTS_AT_K = 0
PRODUCTS_AT_W = 3


def tile_gated_expert_down_d3_kernel(tc, gate, up, router, w_bytes, w_scale, out):
    nc = tc.nc
    with ExitStack() as ctx:
        ctx.enter_context(tc.manual_schedule())
        keep = ctx.enter_context(tc.tile_pool(name="keep", bufs=1))
        work = ctx.enter_context(tc.tile_pool(name="work", bufs=4))
        psum = ctx.enter_context(tc.psum_pool(name="psum", bufs=2))

        gate_rows = gate.rearrange("(p i) f -> i p f", i=NT)
        up_rows = up.rearrange("(p i) f -> i p f", i=NT)
        out_rows = out.rearrange("(p i) d -> i p d", i=NT)
        w_rows = w_bytes.rearrange("(g p t) n -> g p t n", p=P, t=4)

        ws = keep.tile([P, G, 4], F32, name="ws")
        ws_src = w_scale.rearrange("(g p t) o -> p g (t o)", p=P, t=4)
        nc.scalar.dma_start(out=ws[:], in_=ws_src)
        r_in = keep.tile([P, NT], BF16, name="r_in")
        nc.scalar.dma_start(out=r_in[:], in_=router.rearrange("(p i) -> p i", i=NT))
        r = keep.tile([P, NT], F32, name="r")
        nc.scalar.activation(out=r[:], in_=r_in[:], func=ACT.Sigmoid)

        ident = keep.tile([P, P], F32, name="ident")
        make_identity(nc, ident[:])

        g_sb, u_sb, w_sb = [], [], []
        for i in range(NT):
            g_sb.append(keep.tile([P, F], BF16, name="gate%d" % i))
            u_sb.append(keep.tile([P, F], BF16, name="up%d" % i))
        for g in range(G):
            w_sb.append(keep.tile([P, 4, D], U8, name="wbytes%d" % g))

        def load_w(g, n0, n1):
            nc.sync.dma_start(out=w_sb[g][:, :, n0:n1], in_=w_rows[g][:, :, n0:n1])

        def load_half(dst, src, i, j):
            nc.sync.dma_start(out=dst[i][:, 1024 * j : 1024 * (j + 1)], in_=src[i][:, 1024 * j : 1024 * (j + 1)])

        def load_tokens(i, j):
            load_half(g_sb, gate_rows, i, j)
            load_half(u_sb, up_rows, i, j)

        load_w(0, 0, 512)
        load_tokens(0, 0)
        load_w(1, 0, 512)
        load_tokens(0, 1)
        load_w(2, 0, 512)
        load_w(3, 0, 512)
        load_tokens(1, 0)
        load_tokens(1, 1)
        load_w(0, 512, D)
        load_w(1, 512, D)
        load_tokens(2, 0)
        load_tokens(2, 1)
        load_w(2, 512, D)
        load_w(3, 512, D)
        for i in range(3, NT):
            load_tokens(i, 0)
            load_tokens(i, 1)

        h_codes, h_scales, w_codes, w_scales = [], [], [], []
        for i in range(NT):
            h_codes.append(keep.tile([P, 512], U32, name="hcodes%d" % i, align_bytes=64))
            h_scales.append(keep.tile([P, 512], U8, name="hscales%d" % i, align_bytes=64))
        for s in range(len(SLICES)):
            w_codes.append(keep.tile([P, G, SLICES[s][1]], U32, name="wcodes%d" % s, align_bytes=64))
            w_scales.append(keep.tile([P, G, SLICES[s][1]], U8, name="wscales%d" % s, align_bytes=64))

        def turn(src, i, j, tag):
            bank = psum.tile([P, 2, 256], F32, name=tag, bufs=2)
            words = src[i][:].bitcast(F32)
            for q in range(2):
                g = 2 * j + q
                for u in range(2):
                    nc.tensor.transpose(
                        bank[:, u, 128 * q : 128 * (q + 1)], words[:, 256 * g + u : 256 * (g + 1) : 2], ident[:]
                    )
            return bank[:].bitcast(BF16).rearrange("p u (x e) -> p x u e", e=2)

        live = {}

        def turn_half(k):
            i, j = divmod(k, 2)
            live["g", k] = turn(g_sb, i, j, "tg")
            live["u", k] = turn(u_sb, i, j, "tu")

        def silu_half(k):
            sil = work.tile([P, 1024], F32, name="sil", bufs=4)
            silv = sil[:].rearrange("p (x u e) -> p x u e", u=2, e=2)
            nc.scalar.activation(out=silv, in_=live.pop(("g", k)), func=ACT.Silu)
            live["s", k] = silv

        def prod_half(k):
            i, j = divmod(k, 2)
            if j == 0:
                h = work.tile([P, 2048], BF16, name="h", bufs=2, align_bytes=64)
                live["h", i] = h
            hv = live["h", i][:, 1024 * j : 1024 * (j + 1)].rearrange("p (x u e) -> p x u e", u=2, e=2)
            nc.vector.tensor_tensor(out=hv, in0=live.pop(("s", k)), in1=live.pop(("u", k)), op=MULT)

        def quantize_hidden(i):
            nc.vector.quantize_mx(
                out=h_codes[i][:].bitcast(FP8X4), scales=h_scales[i][:], in_=live.pop(("h", i))[:]
            )

        def widen(s, g):
            n0, nw = SLICES[s]
            planes = work.tile([P, 4, nw], BF16, name="planes", bufs=3)
            for t in range(4):
                nc.vector.tensor_scalar(
                    out=planes[:, t, :],
                    in0=w_sb[g][:, t, n0 : n0 + nw].bitcast(FP8),
                    scalar1=ws[:, g, t : t + 1],
                    scalar2=None,
                    op0=MULT,
                )
            mixed = work.tile([P, nw, 4], BF16, name="mixed", bufs=6, align_bytes=64)
            live["p", s, g] = planes
            live["m", s, g] = mixed

        def interleave(s, g, c0, c1, copy):
            planes, mixed = live["p", s, g], live["m", s, g]
            copy(
                out=mixed[:, c0:c1, :].rearrange("p (c i) t -> p c t i", i=4),
                in_=planes[:, :, c0:c1].rearrange("p t (c i) -> p c t i", i=4),
            )

        def quantize_weights(s, g):
            mixed = live.pop(("m", s, g))
            nc.vector.quantize_mx(
                out=w_codes[s][:, g, :].bitcast(FP8X4),
                scales=w_scales[s][:, g, :],
                in_=mixed[:].rearrange("p n t -> p (n t)"),
            )

        def product(i, s):
            n0, nw = SLICES[s]
            acc = psum.tile([P, 512], F32, name="acc", bufs=4)
            for g in range(G):
                nc.tensor.matmul_mx(
                    out=acc[:, :nw],
                    lhsT=h_codes[i][:, 128 * g : 128 * (g + 1)].bitcast(FP8X4),
                    lhsT_scale=h_scales[i][:, 128 * g : 128 * (g + 1)],
                    rhs=w_codes[s][:, g, :].bitcast(FP8X4),
                    rhs_scale=w_scales[s][:, g, :],
                    start=(g == 0),
                    stop=(g == G - 1),
                )
            return acc

        exit_count = [0]

        def finish(i, s, acc):
            n0, nw = SLICES[s]
            res = work.tile([P, 512], F32, name="res", bufs=6)
            if exit_count[0] < SCALAR_EXITS or exit_count[0] % 2 == 0:
                nc.scalar.activation(out=res[:, :nw], in_=acc[:, :nw], func=ACT.Copy, scale=r[:, i : i + 1])
            else:
                nc.vector.tensor_scalar(
                    out=res[:, :nw], in0=acc[:, :nw], scalar1=r[:, i : i + 1], scalar2=None, op0=MULT
                )
            exit_count[0] += 1
            nc.sync.dma_start(out=out_rows[i][:, n0 : n0 + nw], in_=res[:, :nw])

        turned, silued, seen = 0, 0, 0
        hidden_done, slices_done, ready, open_banks = [], [], [], []
        quantized = [0] * len(SLICES)
        later = []

        def run_products(n):
            for pair in ready[:n]:
                open_banks.append((pair, product(*pair)))
                while len(open_banks) > EXIT_LAG:
                    pair2, acc = open_banks.pop(0)
                    finish(*pair2, acc)
            del_n = ready[n:]
            ready.clear()
            ready.extend(del_n)

        def end_hidden(i):
            quantize_hidden(i)
            hidden_done.append(i)
            ready.extend([(i, s) for s in slices_done])

        def end_weights(s, g):
            quantize_weights(s, g)
            quantized[s] += 1
            if quantized[s] == G:
                slices_done.append(s)
                ready.extend([(i, s) for i in hidden_done])

        for n, step in enumerate(STEPS + ["-"] * 4):
            due = [x for x in later if x[0] <= n]
            later = [x for x in later if x[0] > n]
            is_k = step.startswith("k")
            if step != "-":
                k = int(step[1:]) if is_k else -1
                want = min(2 * NT, max(seen + SILU_AHEAD, k + 1))
                while turned < min(2 * NT, max(seen + TURN_AHEAD, want)):
                    turn_half(turned)
                    turned += 1
                while silued < want:
                    silu_half(silued)
                    silued += 1
            if is_k:
                prod_half(k)
                seen = k + 1
                if k % 2 == 1:
                    later.append((n + 1, end_hidden, (k // 2,)))
            elif step != "-":
                s, g = int(step[1:2]), int(step[2:])
                nw = SLICES[s][1]
                widen(s, g)
                c = SCALAR_COLS[s]
                if c > 0:
                    interleave(s, g, 0, c, nc.scalar.copy)
                if c < nw:
                    later.append((n + 1, interleave, (s, g, c, nw, nc.vector.tensor_copy)))
                later.append((n + 4, end_weights, (s, g)))
            for x in due:
                x[1](*x[2])
            run_products(PRODUCTS_AT_K if is_k else PRODUCTS_AT_W)
        run_products(len(ready))
        while open_banks:
            pair2, acc = open_banks.pop(0)
            finish(*pair2, acc)
